import numpy as np
import ml_dtypes


def mxq(x, axis, fmt="e4m3"):
    dtype, down = {"e4m3": (ml_dtypes.float8_e4m3fn, 7), "e5m2": (ml_dtypes.float8_e5m2, 14)}[fmt]
    v = np.moveaxis(np.asarray(x, np.float32).astype(ml_dtypes.bfloat16).astype(np.float64), axis, -1)
    blocks = v.reshape(v.shape[:-1] + (-1, 32))
    amax = np.abs(blocks).max(-1, keepdims=True)
    byte = np.maximum(np.where(amax > 0, np.frexp(amax)[1] - 1 + 127, 0) - down, 1)
    scale = np.exp2(byte - 127.0)
    codes = (blocks / scale).astype(np.float32).astype(dtype).astype(np.float64)
    return np.moveaxis((codes * scale).reshape(v.shape), -1, axis)


WIDE = False


def mx_kscale(k):
    if not WIDE:
        return np.ones(k)
    levels = np.array([10, -10, 5, -5, 0])
    if k % 512:
        return np.exp2(np.random.permutation(np.resize(levels, k // 32))).repeat(32)
    a = np.empty((k // 512, 16))
    for p in range(k // 512):
        a[p, :8] = np.random.permutation(np.resize(levels, 8))
        for g in range(8):
            far = levels[np.abs(levels - a[p, g]) >= 10]
            a[p, g + 8] = far[np.random.randint(len(far))]
    return np.exp2(a.ravel()).repeat(32)


def f64(x):
    return np.asarray(x).astype(np.float64)


def striped(idx):
    return np.tile(idx.reshape(-1, 16).T, (8, 1)).astype(np.uint16)


def unstriped(offs):
    return offs[:16].T.reshape(-1).astype(np.int64)


E2M1 = np.array([0.0, 0.5, 1.0, 1.5, 2.0, 3.0, 4.0, 6.0, -0.0, -0.5, -1.0, -1.5, -2.0, -3.0, -4.0, -6.0])


def pack_weight(w, fmt):
    k, n = w.shape
    w = f64(np.asarray(w, np.float32).astype(ml_dtypes.bfloat16)).reshape(k // 32, 32, n)
    amax = np.abs(w).max(1)
    if fmt == "e4m3":
        byte = np.frexp(amax)[1] - 1 + 127 - 7
    else:
        mant, ex = np.frexp(amax / 6.0)
        byte = np.where(mant > 0.5, ex, ex - 1) + 127
    byte = np.clip(np.where(amax > 0, byte, 1), 1, 254)
    scaled = (w * np.exp2(127.0 - byte)[:, None, :]).reshape(k, n).astype(np.float32)
    by_word = np.ascontiguousarray(scaled.reshape(k // 512, 128, 4, n).transpose(0, 1, 3, 2))
    if fmt == "e4m3":
        words = by_word.astype(ml_dtypes.float8_e4m3fn).view(np.uint8)
    else:
        c = by_word.astype(ml_dtypes.float4_e2m1fn).view(np.uint8) & 0xF
        words = (c[..., 0::2] | (c[..., 1::2] << 4)).reshape(k // 512, 128, 2 * n)
    return np.ascontiguousarray(words), np.ascontiguousarray(byte.astype(np.uint8).reshape(k // 512, 16, n))


def unpack_weight(words, scales, fmt):
    g, _, n = scales.shape
    words = np.ascontiguousarray(words).reshape(g, 128, n, -1)
    if fmt == "e4m3":
        vals = words.view(ml_dtypes.float8_e4m3fn).astype(np.float64)
    else:
        nib = np.empty((g, 128, n, 4), np.uint8)
        nib[..., 0::2] = words & 0xF
        nib[..., 1::2] = words >> 4
        vals = E2M1[nib]
    vals = vals * np.repeat(np.exp2(scales.astype(np.float64) - 127.0), 8, axis=1)[..., None]
    return vals.transpose(0, 1, 3, 2).reshape(g * 512, n)


def gelu(v):
    return 0.5 * v * (1.0 + np.tanh(np.sqrt(2.0 / np.pi) * (v + 0.044715 * v**3)))


K, T, S, H, T3, S2, P = 1536, 4096, 1024, 512, 2048, 512, 512

def setup_inputs():
    n = np.random.standard_normal
    s = mx_kscale(K)[:, None]
    u = mx_kscale(H)[:, None]
    d = {}
    d["tab_words"], d["tab_scales"] = pack_weight(n((K, T)) * s, "e4m3")
    d["tab2_words"], d["tab2_scales"] = pack_weight(n((H, T3)) / H ** 0.5 / u, "e4m3")
    d["w1"] = (n((K, H)) / K ** 0.5 / s).astype(np.float32)
    d["w4_words"], d["w4_scales"] = pack_weight(n((K, H)) / K ** 0.5 / s, "e2m1")
    d["gain"] = (np.exp(0.3 * n(H)) * u[:, 0]).astype(np.float32)
    d["rain"] = n((S2, P)).astype(np.float32)
    d["scen"] = np.exp(0.3 * n(S2)).astype(np.float32)
    d["offs"] = striped(np.random.permutation(T)[:S])
    d["offs2"] = striped(np.random.permutation(T3)[:S2])
    d["pos1"] = striped(np.random.permutation(S)[:P])
    d["pos2"] = striped(np.random.permutation(S)[:P])
    return d

def reference(tab_words, tab_scales, tab2_words, tab2_scales, w1, w4_words, w4_scales,
              gain, rain, scen, offs, offs2, pos1, pos2):
    v = unpack_weight(tab_words, tab_scales, "e4m3")[:, unstriped(offs)]
    v2 = unpack_weight(tab2_words, tab2_scales, "e4m3")[:, unstriped(offs2)]
    w4 = unpack_weight(w4_words, w4_scales, "e2m1")
    w1q = mxq(f64(w1), 0, "e4m3")
    first = np.abs(w1q.T @ v)
    other = np.abs(w4.T @ v)
    h = (first - other) * f64(gain)[:, None]
    hq = mxq(h, 0, "e4m3")
    e = v2.T @ hq
    upper = e[:, unstriped(pos1)]
    lower = e[:, unstriped(pos2)]
    return upper * f64(rain) + lower * f64(scen)[:, None]

@@ -1,0 +1,248 @@
+from contextlib import ExitStack
+
+import concourse.mybir as mybir
+
+K, T, S, H, T3, S2, NP = 1536, 4096, 1024, 512, 2048, 512, 512
+FLOPS = 2 * (2 * K * H * S + H * S2 * S)
+
+F32 = mybir.dt.float32
+BF16 = mybir.dt.bfloat16
+I32 = mybir.dt.int32
+U32 = mybir.dt.uint32
+U16 = mybir.dt.uint16
+U8 = mybir.dt.uint8
+E4M3 = mybir.dt.float8_e4m3fn_x4
+E2M1 = mybir.dt.float4_e2m1fn_x4
+ALU = mybir.AluOpType
+ACT = mybir.ActivationFunctionType
+
+P = 128
+PACK = 4
+PASSES = K // (P * PACK)
+BANK = 512
+HALVES = S // BANK
+CHUNK = 256
+CHUNKS = S // CHUNK
+M_TILES = S2 // P
+
+
+def tile_list_inclinometer_scenario_scores_kernel(
+    tc, tab_words, tab_scales, tab2_words, tab2_scales, w1, w4_words, w4_scales,
+    gain, rain, scen, offs, offs2, pos1, pos2, out,
+):
+    nc = tc.nc
+    with ExitStack() as ctx:
+        lists = ctx.enter_context(tc.tile_pool(name="lists", bufs=1))
+        keep = ctx.enter_context(tc.tile_pool(name="keep", bufs=1))
+        work = ctx.enter_context(tc.tile_pool(name="work", bufs=2))
+        stream = ctx.enter_context(tc.tile_pool(name="stream", bufs=1))
+        psum = ctx.enter_context(tc.psum_pool(name="psum", bufs=1))
+
+        def held(shape, dtype, name):
+            return keep.tile(shape, dtype, name=name, align_bytes=64)
+
+        def streamed(shape, dtype, name, kib):
+            return stream.tile(shape, dtype, name=name, align_bytes=64, offset=kib * 1024)
+
+        def bank(half, t):
+            return psum.tile([P, BANK], F32, name="bank", tag="bank%d" % (half * PACK + t))
+
+        tab_sc = streamed([P, T], U8, "tab_sc", 46)
+        w4_sc_raw = held([P, PASSES * H], U8, "w4_sc_raw")
+        tab2_sc = held([P, T3], U8, "tab2_sc")
+        v_sc_moved = [held([P, S], U8, "v_sc_moved%d" % a) for a in range(1, PASSES)]
+        nc.vector.memset(tab_sc[:].bitcast(I32), 0)
+        for moved in v_sc_moved:
+            nc.vector.memset(moved[:].bitcast(I32), 0)
+        nc.gpsimd.memset(w4_sc_raw[:].bitcast(I32), 0)
+        for q in range(4):
+            nc.gpsimd.dma_start(
+                out=w4_sc_raw[32 * q : 32 * q + 4, :].bitcast(I32),
+                in_=w4_scales[:, 4 * q : 4 * q + 4, :].rearrange("a r c -> r a c").bitcast(I32),
+            )
+        nc.gpsimd.memset(tab2_sc[:].bitcast(I32), 0)
+        for q in range(4):
+            nc.gpsimd.dma_start(
+                out=tab2_sc[32 * q : 32 * q + 4, :].bitcast(I32),
+                in_=tab2_scales[0, 4 * q : 4 * q + 4, :].bitcast(I32),
+            )
+
+        idx = lists.tile([P, S // 16], U16, name="idx")
+        idx2 = lists.tile([P, S2 // 16], U16, name="idx2")
+        upper_pos = lists.tile([P, NP // 16], U16, name="upper_pos")
+        lower_pos = lists.tile([P, NP // 16], U16, name="lower_pos")
+        tab_w = [streamed([P, T], I32, "tab_w%d" % a, 16 * a) for a in range(PASSES)]
+        words = [tab_words[a].rearrange("p t i -> p (t i)").bitcast(I32) for a in range(PASSES)]
+        w4_raw = held([P, PASSES, 2 * H], U8, "w4_raw")
+        gain_sb = held([P, PACK], F32, "gain_sb")
+
+        nc.sync.dma_start(out=tab_w[0][:, : T // 2], in_=words[0][:, : T // 2])
+        nc.sync.dma_start(idx[:], offs)
+        nc.sync.dma_start(out=w4_raw[:].bitcast(I32), in_=w4_words.rearrange("a p b -> p a b").bitcast(I32))
+        for q in range(4):
+            nc.sync.dma_start(
+                out=tab_sc[32 * q : 32 * q + 4 * PASSES, :].bitcast(I32),
+                in_=tab_scales[:, 4 * q : 4 * q + 4, :].bitcast(I32),
+            )
+        nc.sync.dma_start(out=tab_w[0][:, T // 2 :], in_=words[0][:, T // 2 :])
+        nc.sync.dma_start(out=tab_w[1][:], in_=words[1])
+        nc.sync.dma_start(out=gain_sb[:], in_=gain.rearrange("(p t) -> p t", t=PACK))
+        nc.sync.dma_start(idx2[:], offs2)
+
+        w4_w = held([P, PASSES, 2 * H], U8, "w4_w")
+        nc.vector.tensor_copy(
+            out=w4_w[:].bitcast(U16).rearrange("p a (t m) -> p a m t", t=PACK),
+            in_=w4_raw[:].bitcast(U16).rearrange("p a (m t) -> p a m t", t=PACK),
+        )
+        v_sc_packed = held([P, S], U8, "v_sc_packed")
+        nc.vector.tensor_copy(v_sc_packed[:], tab_sc[:].indirect(idx[:]))
+        live = 3 * 32 + 4
+        for a in range(1, PASSES):
+            nc.sync.dma_start(
+                out=v_sc_moved[a - 1][0:live, :].bitcast(I32),
+                in_=v_sc_packed[4 * a : 4 * a + live, :].bitcast(I32),
+            )
+        v_sc = [v_sc_packed] + v_sc_moved
+        nc.sync.dma_start(out=tab_w[2][:], in_=words[2])
+        nc.sync.dma_start(upper_pos[:], pos1)
+        nc.sync.dma_start(lower_pos[:], pos2)
+
+        w4_sc = streamed([P, PASSES, H], U8, "w4_sc", 8)
+        v2_sc = streamed([P, S2], U8, "v2_sc", 26)
+
+        sign = held([P, CHUNK, PACK], BF16, "sign")
+        nc.scalar.activation(out=sign[:], in_=gain_sb[:].unsqueeze(1).to_broadcast([P, CHUNK, PACK]), func=ACT.Sign)
+
+        v_w = [[held([P, BANK], U32, "v_w%d_%d" % (a, u)) for u in range(HALVES)] for a in range(PASSES)]
+        other = [[bank(u, t) for t in range(PACK)] for u in range(HALVES)]
+        for a in range(PASSES):
+            for u in range(HALVES):
+                nc.vector.tensor_copy(
+                    v_w[a][u][:], tab_w[a][:].bitcast(U32).indirect(idx[:, u * BANK // 16 : (u + 1) * BANK // 16])
+                )
+            if a == 0:
+                nc.vector.tensor_copy(
+                    out=w4_sc[:].rearrange("p a (t m) -> p a t m", t=PACK),
+                    in_=w4_sc_raw[:].rearrange("p (a m t) -> p a t m", a=PASSES, t=PACK),
+                )
+            if a == 1:
+                nc.vector.tensor_copy(v2_sc[:], tab2_sc[:].indirect(idx2[:]))
+            for u in range(HALVES):
+                cols = slice(u * BANK, (u + 1) * BANK)
+                for t in range(PACK):
+                    nc.tensor.matmul_mx(
+                        out=other[u][t][:],
+                        lhsT=w4_w[:, a, 2 * P * t : 2 * P * (t + 1)].bitcast(E2M1),
+                        lhsT_scale=w4_sc[:, a, P * t : P * (t + 1)],
+                        rhs=v_w[a][u][:].bitcast(E4M3),
+                        rhs_scale=v_sc[a][:, cols],
+                        start=(a == 0),
+                        stop=(a == PASSES - 1),
+                    )
+        w1_pieces = []
+        for a in range(PASSES):
+            rows = w1[a * P * PACK : (a + 1) * P * PACK, :].rearrange("(p j) c -> p j c", j=PACK)
+            cuts = 2 if a == PASSES - 1 else 1
+            width = H // cuts
+            for u in range(cuts):
+                raw = streamed([P, PACK, width], F32, "w1_raw%d_%d" % (a, u), (0, 10, 18)[a] + 4 * u)
+                nc.sync.dma_start(out=raw[:], in_=rows[:, :, u * width : (u + 1) * width])
+                w1_pieces.append((a, u * width, width, raw))
+
+        tab2_w = streamed([P, T3], I32, "tab2_w", 28)
+        nc.sync.dma_start(out=tab2_w[:], in_=tab2_words[0].rearrange("p t i -> p (t i)").bitcast(I32))
+        rain_sb = streamed([P, M_TILES, NP], F32, "rain_sb", 36)
+        nc.sync.dma_start(out=rain_sb[:], in_=rain.rearrange("(i p) n -> p i n", p=P))
+        scen_sb = streamed([P, M_TILES], F32, "scen_sb", 27)
+        with nc.allow_non_contiguous_dma(reason="one factor a partition"):
+            nc.sync.dma_start(out=scen_sb[:], in_=scen.rearrange("(i p) -> p i", p=P))
+
+        other_abs = [held([P, PACK, CHUNK], F32, "other_abs%d" % c) for c in range(CHUNKS)]
+        for c in range(CHUNKS):
+            u, lo = divmod(c * CHUNK, BANK)
+            for t in range(PACK):
+                nc.scalar.activation(
+                    out=other_abs[c][:, t, :], in_=other[u][t][:, lo : lo + CHUNK], func=ACT.Abs,
+                    scale=gain_sb[:, t : t + 1],
+                )
+
+        w1_bf = [held([P, PACK, P, PACK], BF16, "w1_bf%d" % a) for a in range(PASSES)]
+        w1_w = [held([P, H], U32, "w1_w%d" % a) for a in range(PASSES)]
+        w1_sc = [held([P, H], U8, "w1_sc%d" % a) for a in range(PASSES)]
+        for a, lo, width, raw in w1_pieces:
+            nc.vector.tensor_copy(
+                out=w1_bf[a][:, :, lo // PACK : (lo + width) // PACK, :].rearrange("p t m j -> p m j t"),
+                in_=raw[:].rearrange("p j (m t) -> p m j t", t=PACK),
+            )
+            if lo + width == H:
+                for t0 in range(0, PACK, 2):
+                    nc.vector.quantize_mx(
+                        out=w1_w[a][:, t0 * P : (t0 + 2) * P].bitcast(E4M3),
+                        scales=w1_sc[a][:, t0 * P : (t0 + 2) * P],
+                        in_=w1_bf[a][:, t0 : t0 + 2, :, :].rearrange("p t m j -> p (t m j)"),
+                    )
+        first = [[bank(u, t) for t in range(PACK)] for u in range(HALVES)]
+        for a in range(PASSES):
+            for u in range(HALVES):
+                for t in range(PACK):
+                    nc.tensor.matmul_mx(
+                        out=first[u][t][:],
+                        lhsT=w1_w[a][:, P * t : P * (t + 1)].bitcast(E4M3),
+                        lhsT_scale=w1_sc[a][:, P * t : P * (t + 1)],
+                        rhs=v_w[a][u][:].bitcast(E4M3),
+                        rhs_scale=v_sc[a][:, u * BANK : (u + 1) * BANK],
+                        start=(a == 0),
+                        stop=(a == PASSES - 1),
+                    )
+
+        v2_w = held([P, S2], U32, "v2_w")
+        nc.vector.tensor_copy(v2_w[:], tab2_w[:].bitcast(U32).indirect(idx2[:]))
+
+        h_w = [held([P, CHUNK], U32, "h_w%d" % c) for c in range(CHUNKS)]
+        h_sc = [held([P, CHUNK], U8, "h_sc%d" % c) for c in range(CHUNKS)]
+        for c in range(CHUNKS):
+            u, lo = divmod(c * CHUNK, BANK)
+            first_abs = held([P, PACK, CHUNK], F32, "first_abs%d" % c)
+            for t in range(PACK):
+                nc.scalar.activation(
+                    out=first_abs[:, t, :], in_=first[u][t][:, lo : lo + CHUNK], func=ACT.Abs,
+                    scale=gain_sb[:, t : t + 1],
+                )
+            size_gap = work.tile([P, CHUNK * PACK], BF16, name="size_gap", align_bytes=64)
+            nc.vector.tensor_tensor(
+                out=size_gap[:].rearrange("p (g i t) -> p g t i", i=4, t=PACK),
+                in0=first_abs[:].rearrange("p t (g i) -> p g t i", i=4),
+                in1=other_abs[c][:].rearrange("p t (g i) -> p g t i", i=4),
+                op=ALU.subtract,
+            )
+            h_bf = work.tile([P, CHUNK * PACK], BF16, name="h_bf", align_bytes=64)
+            nc.vector.tensor_tensor(
+                out=h_bf[:], in0=size_gap[:], in1=sign[:].rearrange("p c t -> p (c t)"), op=ALU.mult
+            )
+            nc.vector.quantize_mx(out=h_w[c][:].bitcast(E4M3), scales=h_sc[c][:], in_=h_bf[:])
+
+        scores = [held([P, S], F32, "scores%d" % i) for i in range(M_TILES)]
+        for c in range(CHUNKS):
+            for i in range(M_TILES):
+                acc = bank(c % 2, i)
+                nc.tensor.matmul_mx(
+                    out=acc[:, 0:CHUNK],
+                    lhsT=v2_w[:, P * i : P * (i + 1)].bitcast(E4M3),
+                    lhsT_scale=v2_sc[:, P * i : P * (i + 1)],
+                    rhs=h_w[c][:].bitcast(E4M3),
+                    rhs_scale=h_sc[c][:],
+                    start=True,
+                    stop=True,
+                )
+                nc.scalar.copy(out=scores[i][:, c * CHUNK : (c + 1) * CHUNK], in_=acc[:, 0:CHUNK])
+
+        for i in range(M_TILES):
+            upper = work.tile([P, NP], F32, name="upper")
+            nc.vector.tensor_tensor(upper[:], scores[i][:].indirect(upper_pos[:]), rain_sb[:, i, :], ALU.mult)
+            lower = work.tile([P, NP], F32, name="lower")
+            nc.vector.tensor_copy(lower[:], scores[i][:].indirect(lower_pos[:]))
+            result = held([P, NP], F32, "result%d" % i)
+            nc.vector.scalar_tensor_tensor(
+                out=result[:], in0=lower[:], scalar=scen_sb[:, i : i + 1], in1=upper[:], op0=ALU.mult, op1=ALU.add
+            )
+            nc.sync.dma_start(out=out[P * i : P * (i + 1), :], in_=result[:])

@@ -24,6 +24,7 @@ HALVES = S // BANK
 CHUNK = 256
 CHUNKS = S // CHUNK
 M_TILES = S2 // P
+HEAD = 3 * T // 8
 
 
 def tile_list_inclinometer_scenario_scores_kernel(
@@ -34,7 +35,6 @@ def tile_list_inclinometer_scenario_scores_kernel(
     with ExitStack() as ctx:
         lists = ctx.enter_context(tc.tile_pool(name="lists", bufs=1))
         keep = ctx.enter_context(tc.tile_pool(name="keep", bufs=1))
-        work = ctx.enter_context(tc.tile_pool(name="work", bufs=2))
         stream = ctx.enter_context(tc.tile_pool(name="stream", bufs=1))
         psum = ctx.enter_context(tc.psum_pool(name="psum", bufs=1))
 
@@ -47,7 +47,7 @@ def tile_list_inclinometer_scenario_scores_kernel(
         def bank(half, t):
             return psum.tile([P, BANK], F32, name="bank", tag="bank%d" % (half * PACK + t))
 
-        tab_sc = streamed([P, T], U8, "tab_sc", 46)
+        tab_sc = streamed([P, T], U8, "tab_sc", 48)
         w4_sc_raw = held([P, PASSES * H], U8, "w4_sc_raw")
         tab2_sc = held([P, T3], U8, "tab2_sc")
         v_sc_moved = [held([P, S], U8, "v_sc_moved%d" % a) for a in range(1, PASSES)]
@@ -55,11 +55,6 @@ def tile_list_inclinometer_scenario_scores_kernel(
         for moved in v_sc_moved:
             nc.vector.memset(moved[:].bitcast(I32), 0)
         nc.gpsimd.memset(w4_sc_raw[:].bitcast(I32), 0)
-        for q in range(4):
-            nc.gpsimd.dma_start(
-                out=w4_sc_raw[32 * q : 32 * q + 4, :].bitcast(I32),
-                in_=w4_scales[:, 4 * q : 4 * q + 4, :].rearrange("a r c -> r a c").bitcast(I32),
-            )
         nc.gpsimd.memset(tab2_sc[:].bitcast(I32), 0)
         for q in range(4):
             nc.gpsimd.dma_start(
@@ -71,12 +66,12 @@ def tile_list_inclinometer_scenario_scores_kernel(
         idx2 = lists.tile([P, S2 // 16], U16, name="idx2")
         upper_pos = lists.tile([P, NP // 16], U16, name="upper_pos")
         lower_pos = lists.tile([P, NP // 16], U16, name="lower_pos")
-        tab_w = [streamed([P, T], I32, "tab_w%d" % a, 16 * a) for a in range(PASSES)]
+        tab_w = [streamed([P, T], I32, "tab_w%d" % a, (0, 18, 34)[a]) for a in range(PASSES)]
         words = [tab_words[a].rearrange("p t i -> p (t i)").bitcast(I32) for a in range(PASSES)]
         w4_raw = held([P, PASSES, 2 * H], U8, "w4_raw")
         gain_sb = held([P, PACK], F32, "gain_sb")
 
-        nc.sync.dma_start(out=tab_w[0][:, : T // 2], in_=words[0][:, : T // 2])
+        nc.sync.dma_start(out=tab_w[0][:, : HEAD], in_=words[0][:, : HEAD])
         nc.sync.dma_start(idx[:], offs)
         nc.sync.dma_start(out=w4_raw[:].bitcast(I32), in_=w4_words.rearrange("a p b -> p a b").bitcast(I32))
         for q in range(4):
@@ -84,19 +79,24 @@ def tile_list_inclinometer_scenario_scores_kernel(
                 out=tab_sc[32 * q : 32 * q + 4 * PASSES, :].bitcast(I32),
                 in_=tab_scales[:, 4 * q : 4 * q + 4, :].bitcast(I32),
             )
-        nc.sync.dma_start(out=tab_w[0][:, T // 2 :], in_=words[0][:, T // 2 :])
+        nc.sync.dma_start(out=tab_w[0][:, HEAD :], in_=words[0][:, HEAD :])
+        for q in range(4):
+            nc.sync.dma_start(
+                out=w4_sc_raw[32 * q : 32 * q + 4, :].bitcast(I32),
+                in_=w4_scales[:, 4 * q : 4 * q + 4, :].rearrange("a r c -> r a c").bitcast(I32),
+            )
         nc.sync.dma_start(out=tab_w[1][:], in_=words[1])
         nc.sync.dma_start(out=gain_sb[:], in_=gain.rearrange("(p t) -> p t", t=PACK))
         nc.sync.dma_start(idx2[:], offs2)
 
         w4_w = held([P, PASSES, 2 * H], U8, "w4_w")
         nc.vector.tensor_copy(
-            out=w4_w[:].bitcast(U16).rearrange("p a (t m) -> p a m t", t=PACK),
-            in_=w4_raw[:].bitcast(U16).rearrange("p a (m t) -> p a m t", t=PACK),
+            out=w4_w[:].bitcast(U16).rearrange("p a (t m) -> p a t m", t=PACK),
+            in_=w4_raw[:].bitcast(U16).rearrange("p a (m t) -> p a t m", t=PACK),
         )
         v_sc_packed = held([P, S], U8, "v_sc_packed")
         nc.vector.tensor_copy(v_sc_packed[:], tab_sc[:].indirect(idx[:]))
-        live = 3 * 32 + 4
+        live = 112
         for a in range(1, PASSES):
             nc.sync.dma_start(
                 out=v_sc_moved[a - 1][0:live, :].bitcast(I32),
@@ -149,21 +149,19 @@ def tile_list_inclinometer_scenario_scores_kernel(
                 nc.sync.dma_start(out=raw[:], in_=rows[:, :, u * width : (u + 1) * width])
                 w1_pieces.append((a, u * width, width, raw))
 
-        tab2_w = streamed([P, T3], I32, "tab2_w", 28)
+        tab2_w = streamed([P, T3], I32, "tab2_w", 30)
         nc.sync.dma_start(out=tab2_w[:], in_=tab2_words[0].rearrange("p t i -> p (t i)").bitcast(I32))
-        rain_sb = streamed([P, M_TILES, NP], F32, "rain_sb", 36)
+        rain_sb = streamed([P, M_TILES, NP], F32, "rain_sb", 38)
         nc.sync.dma_start(out=rain_sb[:], in_=rain.rearrange("(i p) n -> p i n", p=P))
         scen_sb = streamed([P, M_TILES], F32, "scen_sb", 27)
         with nc.allow_non_contiguous_dma(reason="one factor a partition"):
             nc.sync.dma_start(out=scen_sb[:], in_=scen.rearrange("(i p) -> p i", p=P))
 
-        other_abs = [held([P, PACK, CHUNK], F32, "other_abs%d" % c) for c in range(CHUNKS)]
-        for c in range(CHUNKS):
-            u, lo = divmod(c * CHUNK, BANK)
+        other_abs = [held([P, PACK, BANK], F32, "other_abs%d" % u) for u in range(HALVES)]
+        for u in range(HALVES):
             for t in range(PACK):
                 nc.scalar.activation(
-                    out=other_abs[c][:, t, :], in_=other[u][t][:, lo : lo + CHUNK], func=ACT.Abs,
-                    scale=gain_sb[:, t : t + 1],
+                    out=other_abs[u][:, t, :], in_=other[u][t][:], func=ACT.Abs, scale=gain_sb[:, t : t + 1]
                 )
 
         w1_bf = [held([P, PACK, P, PACK], BF16, "w1_bf%d" % a) for a in range(PASSES)]
@@ -171,8 +169,8 @@ def tile_list_inclinometer_scenario_scores_kernel(
         w1_sc = [held([P, H], U8, "w1_sc%d" % a) for a in range(PASSES)]
         for a, lo, width, raw in w1_pieces:
             nc.vector.tensor_copy(
-                out=w1_bf[a][:, :, lo // PACK : (lo + width) // PACK, :].rearrange("p t m j -> p m j t"),
-                in_=raw[:].rearrange("p j (m t) -> p m j t", t=PACK),
+                out=w1_bf[a][:, :, lo // PACK : (lo + width) // PACK, :].rearrange("p t m j -> p m t j"),
+                in_=raw[:].rearrange("p j (m t) -> p m t j", t=PACK),
             )
             if lo + width == H:
                 for t0 in range(0, PACK, 2):
@@ -182,8 +180,8 @@ def tile_list_inclinometer_scenario_scores_kernel(
                         in_=w1_bf[a][:, t0 : t0 + 2, :, :].rearrange("p t m j -> p (t m j)"),
                     )
         first = [[bank(u, t) for t in range(PACK)] for u in range(HALVES)]
-        for a in range(PASSES):
-            for u in range(HALVES):
+        for u in range(HALVES):
+            for a in range(PASSES):
                 for t in range(PACK):
                     nc.tensor.matmul_mx(
                         out=first[u][t][:],
@@ -200,7 +198,11 @@ def tile_list_inclinometer_scenario_scores_kernel(
 
         h_w = [held([P, CHUNK], U32, "h_w%d" % c) for c in range(CHUNKS)]
         h_sc = [held([P, CHUNK], U8, "h_sc%d" % c) for c in range(CHUNKS)]
-        for c in range(CHUNKS):
+        size_gap = [held([P, CHUNK * PACK], BF16, "size_gap%d" % c) for c in range(CHUNKS)]
+        h_bf = [held([P, CHUNK * PACK], BF16, "h_bf%d" % c) for c in range(CHUNKS)]
+        scores = [held([P, S], F32, "scores%d" % i) for i in range(M_TILES)]
+
+        def subtract(c):
             u, lo = divmod(c * CHUNK, BANK)
             first_abs = held([P, PACK, CHUNK], F32, "first_abs%d" % c)
             for t in range(PACK):
@@ -208,20 +210,26 @@ def tile_list_inclinometer_scenario_scores_kernel(
                     out=first_abs[:, t, :], in_=first[u][t][:, lo : lo + CHUNK], func=ACT.Abs,
                     scale=gain_sb[:, t : t + 1],
                 )
-            size_gap = work.tile([P, CHUNK * PACK], BF16, name="size_gap", align_bytes=64)
             nc.vector.tensor_tensor(
-                out=size_gap[:].rearrange("p (g i t) -> p g t i", i=4, t=PACK),
+                out=size_gap[c][:].rearrange("p (g i t) -> p g t i", i=4, t=PACK),
                 in0=first_abs[:].rearrange("p t (g i) -> p g t i", i=4),
-                in1=other_abs[c][:].rearrange("p t (g i) -> p g t i", i=4),
+                in1=other_abs[u][:, :, lo : lo + CHUNK].rearrange("p t (g i) -> p g t i", i=4),
                 op=ALU.subtract,
             )
-            h_bf = work.tile([P, CHUNK * PACK], BF16, name="h_bf", align_bytes=64)
-            nc.vector.tensor_tensor(
-                out=h_bf[:], in0=size_gap[:], in1=sign[:].rearrange("p c t -> p (c t)"), op=ALU.mult
-            )
-            nc.vector.quantize_mx(out=h_w[c][:].bitcast(E4M3), scales=h_sc[c][:], in_=h_bf[:])
 
-        scores = [held([P, S], F32, "scores%d" % i) for i in range(M_TILES)]
+        def give_sign(c):
+            nc.vector.tensor_tensor(
+                out=h_bf[c][:], in0=size_gap[c][:], in1=sign[:].rearrange("p c t -> p (c t)"), op=ALU.mult
+            )
+
+        def quantise(c):
+            nc.vector.quantize_mx(out=h_w[c][:].bitcast(E4M3), scales=h_sc[c][:], in_=h_bf[c][:])
+
+        for step in range(CHUNKS + 2):
+            for lag, stage in enumerate((subtract, give_sign, quantise)):
+                if 0 <= step - lag < CHUNKS:
+                    stage(step - lag)
+
         for c in range(CHUNKS):
             for i in range(M_TILES):
                 acc = bank(c % 2, i)
@@ -236,13 +244,27 @@ def tile_list_inclinometer_scenario_scores_kernel(
                 )
                 nc.scalar.copy(out=scores[i][:, c * CHUNK : (c + 1) * CHUNK], in_=acc[:, 0:CHUNK])
 
-        for i in range(M_TILES):
-            upper = work.tile([P, NP], F32, name="upper")
-            nc.vector.tensor_tensor(upper[:], scores[i][:].indirect(upper_pos[:]), rain_sb[:, i, :], ALU.mult)
-            lower = work.tile([P, NP], F32, name="lower")
-            nc.vector.tensor_copy(lower[:], scores[i][:].indirect(lower_pos[:]))
-            result = held([P, NP], F32, "result%d" % i)
+        upper = [held([P, NP], F32, "upper%d" % i) for i in range(M_TILES)]
+        lower = [held([P, NP], F32, "lower%d" % i) for i in range(M_TILES)]
+
+        def pick_upper(i):
+            nc.vector.tensor_tensor(upper[i][:], scores[i][:].indirect(upper_pos[:]), rain_sb[:, i, :], ALU.mult)
+
+        def pick_lower(i):
+            nc.vector.tensor_copy(lower[i][:], scores[i][:].indirect(lower_pos[:]))
+
+        def combine(i, lo, hi):
+            result = held([P, hi - lo], F32, "result%d_%d" % (i, lo))
             nc.vector.scalar_tensor_tensor(
-                out=result[:], in0=lower[:], scalar=scen_sb[:, i : i + 1], in1=upper[:], op0=ALU.mult, op1=ALU.add
+                out=result[:], in0=lower[i][:, lo:hi], scalar=scen_sb[:, i : i + 1], in1=upper[i][:, lo:hi],
+                op0=ALU.mult, op1=ALU.add,
             )
-            nc.sync.dma_start(out=out[P * i : P * (i + 1), :], in_=result[:])
+            nc.sync.dma_start(out=out[P * i : P * (i + 1), lo:hi], in_=result[:])
+
+        for i in range(M_TILES):
+            pick_lower(i)
+            if i > 0:
+                combine(i - 1, 0, NP)
+            pick_upper(i)
+        combine(M_TILES - 1, 0, NP // 2)
+        combine(M_TILES - 1, NP // 2, NP)

@@ -110,9 +110,6 @@ def tile_list_inclinometer_scenario_scores_kernel(
         w4_sc = streamed([P, PASSES, H], U8, "w4_sc", 8)
         v2_sc = streamed([P, S2], U8, "v2_sc", 26)
 
-        sign = held([P, CHUNK, PACK], BF16, "sign")
-        nc.scalar.activation(out=sign[:], in_=gain_sb[:].unsqueeze(1).to_broadcast([P, CHUNK, PACK]), func=ACT.Sign)
-
         v_w = [[held([P, BANK], U32, "v_w%d_%d" % (a, u)) for u in range(HALVES)] for a in range(PASSES)]
         other = [[bank(u, t) for t in range(PACK)] for u in range(HALVES)]
         for a in range(PASSES):
@@ -160,17 +157,25 @@ def tile_list_inclinometer_scenario_scores_kernel(
         other_abs = [held([P, PACK, BANK], F32, "other_abs%d" % u) for u in range(HALVES)]
         for u in range(HALVES):
             for t in range(PACK):
+                nc.scalar.activation(out=other_abs[u][:, t, :], in_=other[u][t][:], func=ACT.Abs)
+        other_gained = [held([P, PACK, BANK], F32, "other_gained%d" % u) for u in range(HALVES)]
+
+        def apply_gain(u):
+            for t in range(PACK):
                 nc.scalar.activation(
-                    out=other_abs[u][:, t, :], in_=other[u][t][:], func=ACT.Abs, scale=gain_sb[:, t : t + 1]
+                    out=other_gained[u][:, t, :], in_=other_abs[u][:, t, :], func=ACT.Copy,
+                    scale=gain_sb[:, t : t + 1],
                 )
+
+        apply_gain(0)
 
         w1_bf = [held([P, PACK, P, PACK], BF16, "w1_bf%d" % a) for a in range(PASSES)]
         w1_w = [held([P, H], U32, "w1_w%d" % a) for a in range(PASSES)]
         w1_sc = [held([P, H], U8, "w1_sc%d" % a) for a in range(PASSES)]
         for a, lo, width, raw in w1_pieces:
             nc.vector.tensor_copy(
-                out=w1_bf[a][:, :, lo // PACK : (lo + width) // PACK, :].rearrange("p t m j -> p m t j"),
-                in_=raw[:].rearrange("p j (m t) -> p m t j", t=PACK),
+                out=w1_bf[a][:, :, lo // PACK : (lo + width) // PACK, :].rearrange("p t m j -> p m j t"),
+                in_=raw[:].rearrange("p j (m t) -> p m j t", t=PACK),
             )
             if lo + width == H:
                 for t0 in range(0, PACK, 2):
@@ -198,40 +203,39 @@ def tile_list_inclinometer_scenario_scores_kernel(
 
         h_w = [held([P, CHUNK], U32, "h_w%d" % c) for c in range(CHUNKS)]
         h_sc = [held([P, CHUNK], U8, "h_sc%d" % c) for c in range(CHUNKS)]
-        size_gap = [held([P, CHUNK * PACK], BF16, "size_gap%d" % c) for c in range(CHUNKS)]
+        h_rows = [held([P, PACK, CHUNK], BF16, "h_rows%d" % c) for c in range(CHUNKS)]
         h_bf = [held([P, CHUNK * PACK], BF16, "h_bf%d" % c) for c in range(CHUNKS)]
         scores = [held([P, S], F32, "scores%d" % i) for i in range(M_TILES)]
 
         def subtract(c):
             u, lo = divmod(c * CHUNK, BANK)
+            if u == 1 and lo == 0:
+                apply_gain(1)
             first_abs = held([P, PACK, CHUNK], F32, "first_abs%d" % c)
             for t in range(PACK):
-                nc.scalar.activation(
-                    out=first_abs[:, t, :], in_=first[u][t][:, lo : lo + CHUNK], func=ACT.Abs,
-                    scale=gain_sb[:, t : t + 1],
+                nc.scalar.activation(out=first_abs[:, t, :], in_=first[u][t][:, lo : lo + CHUNK], func=ACT.Abs)
+                nc.vector.scalar_tensor_tensor(
+                    out=h_rows[c][:, t, :], in0=first_abs[:, t, :], scalar=gain_sb[:, t : t + 1],
+                    in1=other_gained[u][:, t, lo : lo + CHUNK], op0=ALU.mult, op1=ALU.subtract,
                 )
-            nc.vector.tensor_tensor(
-                out=size_gap[c][:].rearrange("p (g i t) -> p g t i", i=4, t=PACK),
-                in0=first_abs[:].rearrange("p t (g i) -> p g t i", i=4),
-                in1=other_abs[u][:, :, lo : lo + CHUNK].rearrange("p t (g i) -> p g t i", i=4),
-                op=ALU.subtract,
-            )
 
-        def give_sign(c):
-            nc.vector.tensor_tensor(
-                out=h_bf[c][:], in0=size_gap[c][:], in1=sign[:].rearrange("p c t -> p (c t)"), op=ALU.mult
+        def interleave(c):
+            copy = nc.scalar.copy if 0 < c < CHUNKS - 1 else nc.vector.tensor_copy
+            copy(
+                out=h_bf[c][:].rearrange("p (g i t) -> p g t i", i=4, t=PACK),
+                in_=h_rows[c][:].rearrange("p t (g i) -> p g t i", i=4),
             )
 
         def quantise(c):
             nc.vector.quantize_mx(out=h_w[c][:].bitcast(E4M3), scales=h_sc[c][:], in_=h_bf[c][:])
 
         for step in range(CHUNKS + 2):
-            for lag, stage in enumerate((subtract, give_sign, quantise)):
+            for lag, stage in enumerate((subtract, interleave, quantise)):
                 if 0 <= step - lag < CHUNKS:
                     stage(step - lag)
 
-        for c in range(CHUNKS):
-            for i in range(M_TILES):
+        for i in range(M_TILES):
+            for c in range(CHUNKS):
                 acc = bank(c % 2, i)
                 nc.tensor.matmul_mx(
                     out=acc[:, 0:CHUNK],

from contextlib import ExitStack

import concourse.mybir as mybir

K, T, S, H, T3, S2, NP = 1536, 4096, 1024, 512, 2048, 512, 512
FLOPS = 2 * (2 * K * H * S + H * S2 * S)

F32 = mybir.dt.float32
BF16 = mybir.dt.bfloat16
I32 = mybir.dt.int32
U32 = mybir.dt.uint32
U16 = mybir.dt.uint16
U8 = mybir.dt.uint8
E4M3 = mybir.dt.float8_e4m3fn_x4
E2M1 = mybir.dt.float4_e2m1fn_x4
ALU = mybir.AluOpType
ACT = mybir.ActivationFunctionType

P = 128
PACK = 4
PASSES = K // (P * PACK)
BANK = 512
HALVES = S // BANK
CHUNK = 256
CHUNKS = S // CHUNK
M_TILES = S2 // P
HEAD = 3 * T // 8


def tile_list_inclinometer_scenario_scores_kernel(
    tc, tab_words, tab_scales, tab2_words, tab2_scales, w1, w4_words, w4_scales,
    gain, rain, scen, offs, offs2, pos1, pos2, out,
):
    nc = tc.nc
    with ExitStack() as ctx:
        lists = ctx.enter_context(tc.tile_pool(name="lists", bufs=1))
        keep = ctx.enter_context(tc.tile_pool(name="keep", bufs=1))
        stream = ctx.enter_context(tc.tile_pool(name="stream", bufs=1))
        psum = ctx.enter_context(tc.psum_pool(name="psum", bufs=1))

        def held(shape, dtype, name):
            return keep.tile(shape, dtype, name=name, align_bytes=64)

        def streamed(shape, dtype, name, kib):
            return stream.tile(shape, dtype, name=name, align_bytes=64, offset=kib * 1024)

        def bank(half, t):
            return psum.tile([P, BANK], F32, name="bank", tag="bank%d" % (half * PACK + t))

        tab_sc = streamed([P, T], U8, "tab_sc", 48)
        w4_sc_raw = held([P, PASSES * H], U8, "w4_sc_raw")
        tab2_sc = held([P, T3], U8, "tab2_sc")
        v_sc_moved = [held([P, S], U8, "v_sc_moved%d" % a) for a in range(1, PASSES)]
        nc.vector.memset(tab_sc[:].bitcast(I32), 0)
        for moved in v_sc_moved:
            nc.vector.memset(moved[:].bitcast(I32), 0)
        nc.gpsimd.memset(w4_sc_raw[:].bitcast(I32), 0)
        nc.gpsimd.memset(tab2_sc[:].bitcast(I32), 0)
        for q in range(4):
            nc.gpsimd.dma_start(
                out=tab2_sc[32 * q : 32 * q + 4, :].bitcast(I32),
                in_=tab2_scales[0, 4 * q : 4 * q + 4, :].bitcast(I32),
            )

        idx = lists.tile([P, S // 16], U16, name="idx")
        idx2 = lists.tile([P, S2 // 16], U16, name="idx2")
        upper_pos = lists.tile([P, NP // 16], U16, name="upper_pos")
        lower_pos = lists.tile([P, NP // 16], U16, name="lower_pos")
        tab_w = [streamed([P, T], I32, "tab_w%d" % a, (0, 18, 34)[a]) for a in range(PASSES)]
        words = [tab_words[a].rearrange("p t i -> p (t i)").bitcast(I32) for a in range(PASSES)]
        w4_raw = held([P, PASSES, 2 * H], U8, "w4_raw")
        gain_sb = held([P, PACK], F32, "gain_sb")

        nc.sync.dma_start(out=tab_w[0][:, : HEAD], in_=words[0][:, : HEAD])
        nc.sync.dma_start(idx[:], offs)
        nc.sync.dma_start(out=w4_raw[:].bitcast(I32), in_=w4_words.rearrange("a p b -> p a b").bitcast(I32))
        for q in range(4):
            nc.sync.dma_start(
                out=tab_sc[32 * q : 32 * q + 4 * PASSES, :].bitcast(I32),
                in_=tab_scales[:, 4 * q : 4 * q + 4, :].bitcast(I32),
            )
        nc.sync.dma_start(out=tab_w[0][:, HEAD :], in_=words[0][:, HEAD :])
        for q in range(4):
            nc.sync.dma_start(
                out=w4_sc_raw[32 * q : 32 * q + 4, :].bitcast(I32),
                in_=w4_scales[:, 4 * q : 4 * q + 4, :].rearrange("a r c -> r a c").bitcast(I32),
            )
        nc.sync.dma_start(out=tab_w[1][:], in_=words[1])
        nc.sync.dma_start(out=gain_sb[:], in_=gain.rearrange("(p t) -> p t", t=PACK))
        nc.sync.dma_start(idx2[:], offs2)

        w4_w = held([P, PASSES, 2 * H], U8, "w4_w")
        nc.vector.tensor_copy(
            out=w4_w[:].bitcast(U16).rearrange("p a (t m) -> p a t m", t=PACK),
            in_=w4_raw[:].bitcast(U16).rearrange("p a (m t) -> p a t m", t=PACK),
        )
        v_sc_packed = held([P, S], U8, "v_sc_packed")
        nc.vector.tensor_copy(v_sc_packed[:], tab_sc[:].indirect(idx[:]))
        live = 112
        for a in range(1, PASSES):
            nc.sync.dma_start(
                out=v_sc_moved[a - 1][0:live, :].bitcast(I32),
                in_=v_sc_packed[4 * a : 4 * a + live, :].bitcast(I32),
            )
        v_sc = [v_sc_packed] + v_sc_moved
        nc.sync.dma_start(out=tab_w[2][:], in_=words[2])
        nc.sync.dma_start(upper_pos[:], pos1)
        nc.sync.dma_start(lower_pos[:], pos2)

        w4_sc = streamed([P, PASSES, H], U8, "w4_sc", 8)
        v2_sc = streamed([P, S2], U8, "v2_sc", 26)

        v_w = [[held([P, BANK], U32, "v_w%d_%d" % (a, u)) for u in range(HALVES)] for a in range(PASSES)]
        other = [[bank(u, t) for t in range(PACK)] for u in range(HALVES)]
        for a in range(PASSES):
            for u in range(HALVES):
                nc.vector.tensor_copy(
                    v_w[a][u][:], tab_w[a][:].bitcast(U32).indirect(idx[:, u * BANK // 16 : (u + 1) * BANK // 16])
                )
            if a == 0:
                nc.vector.tensor_copy(
                    out=w4_sc[:].rearrange("p a (t m) -> p a t m", t=PACK),
                    in_=w4_sc_raw[:].rearrange("p (a m t) -> p a t m", a=PASSES, t=PACK),
                )
            if a == 1:
                nc.vector.tensor_copy(v2_sc[:], tab2_sc[:].indirect(idx2[:]))
            for u in range(HALVES):
                cols = slice(u * BANK, (u + 1) * BANK)
                for t in range(PACK):
                    nc.tensor.matmul_mx(
                        out=other[u][t][:],
                        lhsT=w4_w[:, a, 2 * P * t : 2 * P * (t + 1)].bitcast(E2M1),
                        lhsT_scale=w4_sc[:, a, P * t : P * (t + 1)],
                        rhs=v_w[a][u][:].bitcast(E4M3),
                        rhs_scale=v_sc[a][:, cols],
                        start=(a == 0),
                        stop=(a == PASSES - 1),
                    )
        w1_pieces = []
        for a in range(PASSES):
            rows = w1[a * P * PACK : (a + 1) * P * PACK, :].rearrange("(p j) c -> p j c", j=PACK)
            cuts = 2 if a == PASSES - 1 else 1
            width = H // cuts
            for u in range(cuts):
                raw = streamed([P, PACK, width], F32, "w1_raw%d_%d" % (a, u), (0, 10, 18)[a] + 4 * u)
                nc.sync.dma_start(out=raw[:], in_=rows[:, :, u * width : (u + 1) * width])
                w1_pieces.append((a, u * width, width, raw))

        tab2_w = streamed([P, T3], I32, "tab2_w", 30)
        nc.sync.dma_start(out=tab2_w[:], in_=tab2_words[0].rearrange("p t i -> p (t i)").bitcast(I32))
        rain_sb = streamed([P, M_TILES, NP], F32, "rain_sb", 38)
        nc.sync.dma_start(out=rain_sb[:], in_=rain.rearrange("(i p) n -> p i n", p=P))
        scen_sb = streamed([P, M_TILES], F32, "scen_sb", 27)
        with nc.allow_non_contiguous_dma(reason="one factor a partition"):
            nc.sync.dma_start(out=scen_sb[:], in_=scen.rearrange("(i p) -> p i", p=P))

        other_abs = [held([P, PACK, BANK], F32, "other_abs%d" % u) for u in range(HALVES)]
        for u in range(HALVES):
            for t in range(PACK):
                nc.scalar.activation(out=other_abs[u][:, t, :], in_=other[u][t][:], func=ACT.Abs)
        other_gained = [held([P, PACK, BANK], F32, "other_gained%d" % u) for u in range(HALVES)]

        def apply_gain(u):
            for t in range(PACK):
                nc.scalar.activation(
                    out=other_gained[u][:, t, :], in_=other_abs[u][:, t, :], func=ACT.Copy,
                    scale=gain_sb[:, t : t + 1],
                )

        apply_gain(0)

        w1_bf = [held([P, PACK, P, PACK], BF16, "w1_bf%d" % a) for a in range(PASSES)]
        w1_w = [held([P, H], U32, "w1_w%d" % a) for a in range(PASSES)]
        w1_sc = [held([P, H], U8, "w1_sc%d" % a) for a in range(PASSES)]
        for a, lo, width, raw in w1_pieces:
            nc.vector.tensor_copy(
                out=w1_bf[a][:, :, lo // PACK : (lo + width) // PACK, :].rearrange("p t m j -> p m j t"),
                in_=raw[:].rearrange("p j (m t) -> p m j t", t=PACK),
            )
            if lo + width == H:
                for t0 in range(0, PACK, 2):
                    nc.vector.quantize_mx(
                        out=w1_w[a][:, t0 * P : (t0 + 2) * P].bitcast(E4M3),
                        scales=w1_sc[a][:, t0 * P : (t0 + 2) * P],
                        in_=w1_bf[a][:, t0 : t0 + 2, :, :].rearrange("p t m j -> p (t m j)"),
                    )
        first = [[bank(u, t) for t in range(PACK)] for u in range(HALVES)]
        for u in range(HALVES):
            for a in range(PASSES):
                for t in range(PACK):
                    nc.tensor.matmul_mx(
                        out=first[u][t][:],
                        lhsT=w1_w[a][:, P * t : P * (t + 1)].bitcast(E4M3),
                        lhsT_scale=w1_sc[a][:, P * t : P * (t + 1)],
                        rhs=v_w[a][u][:].bitcast(E4M3),
                        rhs_scale=v_sc[a][:, u * BANK : (u + 1) * BANK],
                        start=(a == 0),
                        stop=(a == PASSES - 1),
                    )

        v2_w = held([P, S2], U32, "v2_w")
        nc.vector.tensor_copy(v2_w[:], tab2_w[:].bitcast(U32).indirect(idx2[:]))

        h_w = [held([P, CHUNK], U32, "h_w%d" % c) for c in range(CHUNKS)]
        h_sc = [held([P, CHUNK], U8, "h_sc%d" % c) for c in range(CHUNKS)]
        h_rows = [held([P, PACK, CHUNK], BF16, "h_rows%d" % c) for c in range(CHUNKS)]
        h_bf = [held([P, CHUNK * PACK], BF16, "h_bf%d" % c) for c in range(CHUNKS)]
        scores = [held([P, S], F32, "scores%d" % i) for i in range(M_TILES)]

        def subtract(c):
            u, lo = divmod(c * CHUNK, BANK)
            if u == 1 and lo == 0:
                apply_gain(1)
            first_abs = held([P, PACK, CHUNK], F32, "first_abs%d" % c)
            for t in range(PACK):
                nc.scalar.activation(out=first_abs[:, t, :], in_=first[u][t][:, lo : lo + CHUNK], func=ACT.Abs)
                nc.vector.scalar_tensor_tensor(
                    out=h_rows[c][:, t, :], in0=first_abs[:, t, :], scalar=gain_sb[:, t : t + 1],
                    in1=other_gained[u][:, t, lo : lo + CHUNK], op0=ALU.mult, op1=ALU.subtract,
                )

        def interleave(c):
            copy = nc.scalar.copy if 0 < c < CHUNKS - 1 else nc.vector.tensor_copy
            copy(
                out=h_bf[c][:].rearrange("p (g i t) -> p g t i", i=4, t=PACK),
                in_=h_rows[c][:].rearrange("p t (g i) -> p g t i", i=4),
            )

        def quantise(c):
            nc.vector.quantize_mx(out=h_w[c][:].bitcast(E4M3), scales=h_sc[c][:], in_=h_bf[c][:])

        for step in range(CHUNKS + 2):
            for lag, stage in enumerate((subtract, interleave, quantise)):
                if 0 <= step - lag < CHUNKS:
                    stage(step - lag)

        for i in range(M_TILES):
            for c in range(CHUNKS):
                acc = bank(c % 2, i)
                nc.tensor.matmul_mx(
                    out=acc[:, 0:CHUNK],
                    lhsT=v2_w[:, P * i : P * (i + 1)].bitcast(E4M3),
                    lhsT_scale=v2_sc[:, P * i : P * (i + 1)],
                    rhs=h_w[c][:].bitcast(E4M3),
                    rhs_scale=h_sc[c][:],
                    start=True,
                    stop=True,
                )
                nc.scalar.copy(out=scores[i][:, c * CHUNK : (c + 1) * CHUNK], in_=acc[:, 0:CHUNK])

        upper = [held([P, NP], F32, "upper%d" % i) for i in range(M_TILES)]
        lower = [held([P, NP], F32, "lower%d" % i) for i in range(M_TILES)]

        def pick_upper(i):
            nc.vector.tensor_tensor(upper[i][:], scores[i][:].indirect(upper_pos[:]), rain_sb[:, i, :], ALU.mult)

        def pick_lower(i):
            nc.vector.tensor_copy(lower[i][:], scores[i][:].indirect(lower_pos[:]))

        def combine(i, lo, hi):
            result = held([P, hi - lo], F32, "result%d_%d" % (i, lo))
            nc.vector.scalar_tensor_tensor(
                out=result[:], in0=lower[i][:, lo:hi], scalar=scen_sb[:, i : i + 1], in1=upper[i][:, lo:hi],
                op0=ALU.mult, op1=ALU.add,
            )
            nc.sync.dma_start(out=out[P * i : P * (i + 1), lo:hi], in_=result[:])

        for i in range(M_TILES):
            pick_lower(i)
            if i > 0:
                combine(i - 1, 0, NP)
            pick_upper(i)
        combine(M_TILES - 1, 0, NP // 2)
        combine(M_TILES - 1, NP // 2, NP)
